import numpy as np
import ml_dtypes


def mxq(x, axis, fmt="e4m3"):
    dtype, down = {"e4m3": (ml_dtypes.float8_e4m3fn, 7), "e5m2": (ml_dtypes.float8_e5m2, 14)}[fmt]
    v = np.moveaxis(np.asarray(x, np.float32).astype(ml_dtypes.bfloat16).astype(np.float64), axis, -1)
    blocks = v.reshape(v.shape[:-1] + (-1, 32))
    amax = np.abs(blocks).max(-1, keepdims=True)
    byte = np.maximum(np.where(amax > 0, np.frexp(amax)[1] - 1 + 127, 0) - down, 1)
    scale = np.exp2(byte - 127.0)
    codes = (blocks / scale).astype(np.float32).astype(dtype).astype(np.float64)
    return np.moveaxis((codes * scale).reshape(v.shape), -1, axis)


WIDE = False


def mx_kscale(k):
    if not WIDE:
        return np.ones(k)
    levels = np.array([10, -10, 5, -5, 0])
    if k % 512:
        return np.exp2(np.random.permutation(np.resize(levels, k // 32))).repeat(32)
    a = np.empty((k // 512, 16))
    for p in range(k // 512):
        a[p, :8] = np.random.permutation(np.resize(levels, 8))
        for g in range(8):
            far = levels[np.abs(levels - a[p, g]) >= 10]
            a[p, g + 8] = far[np.random.randint(len(far))]
    return np.exp2(a.ravel()).repeat(32)


def f64(x):
    return np.asarray(x).astype(np.float64)


def striped(idx):
    return np.tile(idx.reshape(-1, 16).T, (8, 1)).astype(np.uint16)


def unstriped(offs):
    return offs[:16].T.reshape(-1).astype(np.int64)


def pack_weight(w):
    k, n = w.shape
    w = f64(np.asarray(w, np.float32).astype(ml_dtypes.bfloat16)).reshape(k // 32, 32, n)
    amax = np.abs(w).max(1)
    byte = np.clip(np.where(amax > 0, np.frexp(amax)[1] - 1 + 127 - 7, 1), 1, 254)
    scaled = (w * np.exp2(127.0 - byte)[:, None, :]).reshape(k, n).astype(np.float32)
    words = np.ascontiguousarray(scaled.reshape(k // 512, 128, 4, n).transpose(0, 1, 3, 2)).astype(ml_dtypes.float8_e4m3fn).view(np.uint8)
    return words, np.ascontiguousarray(byte.astype(np.uint8).reshape(k // 512, 16, n))


def unpack_weight(words, scales):
    g, p, n, _ = words.shape
    vals = np.ascontiguousarray(words).view(ml_dtypes.float8_e4m3fn).astype(np.float64) * np.repeat(np.exp2(scales.astype(np.float64) - 127.0), 8, axis=1)[..., None]
    return vals.transpose(0, 1, 3, 2).reshape(g * 512, n)


K, T, D, S, V, H, N = 512, 2048, 2, 1024, 512, 1024, 128
P = 2 ** 7


def setup_inputs():
    n = np.random.standard_normal
    s = mx_kscale(K)[:, None]
    u = mx_kscale(H)
    q = np.random.permutation(S)
    packed = pack_weight(n((K, T)) * s)
    return {
        "x_words": packed[0],
        "x_scales": packed[1],
        "w1": (n((K, H)) / np.sqrt(K) / s * u).astype(np.float32),
        "w2": (n((H, N)) / np.sqrt(H) / u[:, None]).astype(np.float32),
        "gate": np.tile(np.random.uniform(0.2, 1.0, (D, 1, V)) / np.sqrt(D), (1, P, 1)).astype(np.float32),
        "offs": striped(np.random.permutation(T)[:S]),
        "pos1": striped(q[:V]),
        "pos2": striped(q[V:]),
    }


def reference(x_words, x_scales, w1, w2, gate, offs, pos1, pos2):
    h = mxq(f64(w1), 0, "e4m3").T @ unpack_weight(x_words, x_scales)[:, unstriped(offs)]
    z = sum(f64(gate)[d, :1] * h[:, unstriped(p)] for d, p in enumerate((pos1, pos2)))
    return mxq(f64(w2), 0, "e4m3").T @ mxq(z, 0, "e4m3")

@@ -1,0 +1,233 @@
+from contextlib import ExitStack
+
+import concourse.mybir as mybir
+
+K, T, S, V, H, N = 512, 2048, 1024, 512, 1024, 128
+FLOPS = 2 * K * H * S + 2 * H * N * V
+
+F32 = mybir.dt.float32
+BF16 = mybir.dt.bfloat16
+I32 = mybir.dt.int32
+U32 = mybir.dt.uint32
+U16 = mybir.dt.uint16
+U8 = mybir.dt.uint8
+FP8X4 = mybir.dt.float8_e4m3fn_x4
+MULT = mybir.AluOpType.mult
+
+P = 128
+BANK = 512
+TILES = H // P
+VT = V // P
+X_PIECES = ((0, 512), (512, 768), (768, 1024))
+W1_LOADS = ((0, 1), (1, 2), (2, 4), (4, 8))
+
+
+def tile_picked_sage_none_p_kernel(
+    tc, x_words, x_scales, w1, w2, gate, offs, pos1, pos2, out
+):
+    nc = tc.nc
+    with ExitStack() as ctx:
+        keep = ctx.enter_context(tc.tile_pool(name="keep", bufs=1))
+        loads = ctx.enter_context(tc.tile_pool(name="loads", bufs=1))
+        ring = ctx.enter_context(tc.tile_pool(name="ring", bufs=4))
+        psum = ctx.enter_context(tc.psum_pool(name="psum", bufs=1))
+        banks = [psum.tile([P, BANK], F32, name=f"bank{i}") for i in range(8)]
+
+        offs_t = keep.tile([P, S // 16], U16, name="offs_t")
+        pos_t = [keep.tile([P, V // 16], U16, name=f"pos{d}_t") for d in range(2)]
+        scale_store = keep.tile([P, T], U8, name="scale_store")
+        ident = keep.tile([P, P], F32, name="ident")
+        zeros = loads.tile([P, P], F32, name="zeros", offset=4 * T - 2 * P)
+        nc.vector.memset(scale_store[:].bitcast(I32), 0)
+        nc.gpsimd.memset(zeros[:], 0.0)
+        nc.gpsimd.affine_select(
+            out=ident[:],
+            in_=zeros[:],
+            compare_op=mybir.AluOpType.not_equal,
+            fill=1.0,
+            base=0,
+            pattern=[[-1, P]],
+            channel_multiplier=1,
+        )
+        word_store = loads.tile([P, T], I32, name="word_store", offset=0)
+        staged = loads.tile([P, 4 * H + 2 * V + 8 * N], F32, name="staged", offset=4 * T)
+        w1_raw = [staged[:, 4 * a * P : 4 * b * P].rearrange("p (j c) -> p j c", j=4) for a, b in W1_LOADS]
+        gates = staged[:, 4 * H : 4 * H + 2 * V].rearrange("p (d v) -> p d v", d=2)
+        w2_raw = staged[:, 4 * H + 2 * V :].rearrange("p (b j m) -> p b j m", b=2, j=4)
+
+        nc.sync.dma_start(offs_t[:], offs)
+        nc.sync.dma_start(pos_t[0][:], pos1)
+        nc.sync.dma_start(pos_t[1][:], pos2)
+        for q in range(4):
+            nc.sync.dma_start(
+                scale_store[32 * q : 32 * q + 4, :].bitcast(I32), x_scales[0, 4 * q : 4 * q + 4, :].bitcast(I32)
+            )
+        nc.sync.dma_start(word_store[:], x_words[0].rearrange("p c r -> p (c r)").bitcast(I32))
+        w1_rows = w1.rearrange("(p j) c -> p j c", j=4)
+
+        def load_w1(i):
+            a, b = W1_LOADS[i]
+            nc.sync.dma_start(w1_raw[i], w1_rows[:, :, a * P : b * P])
+
+        load_w1(0)
+        nc.sync.dma_start(gates, gate.rearrange("d p v -> p d v"))
+        load_w1(1)
+        load_w1(2)
+        load_w1(3)
+        nc.sync.dma_start(w2_raw, w2.rearrange("(b p j) m -> p b j m", b=2, j=4))
+
+        x_bytes = keep.tile([P, S], U8, name="x_bytes", align_bytes=64)
+        x_codes = []
+
+        def gather_words(i, tag):
+            a, b = X_PIECES[i]
+            codes = keep.tile([P, b - a], U32, name=f"x_codes{i}", tag=tag, align_bytes=64)
+            nc.vector.tensor_copy(codes[:], word_store[:].bitcast(U32).indirect(offs_t[:, a // 16 : b // 16]))
+            x_codes.append(codes)
+
+        w1_codes = [keep.tile([P, P], U32, name=f"w1_codes{c}", align_bytes=64) for c in range(TILES)]
+        w1_scales = [keep.tile([P, P], U8, name=f"w1_scales{c}", align_bytes=64) for c in range(TILES)]
+        h = [keep.tile([P, S], F32, name=f"h{c}") for c in range(TILES)]
+        z_rows = [[keep.tile([P, BANK], BF16, name=f"z_rows{b}_{u}") for u in range(VT)] for b in range(2)]
+        z_codes = [keep.tile([P, V], U32, name=f"z_codes{b}", align_bytes=64) for b in range(2)]
+        z_scales = [keep.tile([P, V], U8, name=f"z_scales{b}", align_bytes=64) for b in range(2)]
+        w2_codes = keep.tile([P, 2 * N], U32, name="w2_codes", align_bytes=64)
+        w2_scales = keep.tile([P, 2 * N], U8, name="w2_scales", align_bytes=64)
+
+        def quantize_w1(c, pool, tag):
+            i = max(n for n, (a, b) in enumerate(W1_LOADS) if a <= c)
+            col = (c - W1_LOADS[i][0]) * P
+            grouped = pool.tile([P, P, 4], BF16, name="w1_grouped", tag=tag, align_bytes=64)
+            nc.scalar.copy(grouped[:], w1_raw[i][:, :, col : col + P].rearrange("p j c -> p c j"))
+            nc.vector.quantize_mx(
+                w1_codes[c][:].bitcast(FP8X4), w1_scales[c][:], grouped[:].rearrange("p c j -> p (c j)")
+            )
+
+        def quantize_w2():
+            grouped = keep.tile([P, 2, N, 4], BF16, name="w2_grouped", align_bytes=64)
+            nc.scalar.copy(grouped[:], w2_raw.rearrange("p b j m -> p b m j"))
+            nc.vector.quantize_mx(
+                w2_codes[:].bitcast(FP8X4), w2_scales[:], grouped[:].rearrange("p b m j -> p (b m j)")
+            )
+
+        def multiply(c, i, dst):
+            a, b = X_PIECES[i]
+            nc.tensor.matmul_mx(
+                dst,
+                lhsT=w1_codes[c][:].bitcast(FP8X4),
+                lhsT_scale=w1_scales[c][:],
+                rhs=x_codes[i][:].bitcast(FP8X4),
+                rhs_scale=x_bytes[:, a:b],
+                start=True,
+                stop=True,
+            )
+
+        def project(c):
+            low, high = banks[2 * (c % 2)], banks[2 * (c % 2) + 1]
+            multiply(c, 0, low[:])
+            nc.scalar.copy(h[c][:, :BANK], low[:])
+            multiply(c, 1, high[:, :256])
+            multiply(c, 2, high[:, 256:])
+            nc.scalar.copy(h[c][:, BANK:], high[:])
+
+        def project_first():
+            multiply(0, 0, banks[0][:])
+            nc.scalar.copy(h[0][:, :BANK], banks[0][:])
+            multiply(0, 1, banks[1][:, :256])
+            nc.scalar.copy(h[0][:, 512:768], banks[1][:, :256])
+            multiply(0, 2, banks[4][:, :256])
+            nc.vector.tensor_copy(h[0][:, 768:], banks[4][:, :256])
+
+        def gather(c, u0, u1):
+            terms = []
+            for d in range(2):
+                term = ring.tile([P, (u1 - u0) * P], F32, name=f"term{d}")
+                nc.vector.tensor_tensor(
+                    term[:],
+                    h[c][:].indirect(pos_t[d][:, 8 * u0 : 8 * u1]),
+                    gates[:, d, u0 * P : u1 * P],
+                    MULT,
+                )
+                terms.append(term)
+            return terms
+
+        def add_turned(c, terms, u0, u1, bank):
+            for u in range(u0, u1):
+                for d in range(2):
+                    nc.tensor.matmul(
+                        bank[:, (u - u0) * P : (u - u0 + 1) * P],
+                        lhsT=terms[d][:, (u - u0) * P : (u - u0 + 1) * P],
+                        rhs=ident[:],
+                        start=(d == 0),
+                        stop=(d == 1),
+                        is_transpose=True,
+                    )
+            for u in range(u0, u1):
+                dst = z_rows[c // 4][u][:].rearrange("v (w q e) -> v w q e", w=2, e=2)
+                nc.scalar.copy(
+                    dst[:, :, 32 * (c % 4) : 32 * (c % 4 + 1), :],
+                    bank[:, (u - u0) * P : (u - u0 + 1) * P].rearrange("v (q w e) -> v w q e", w=2, e=2),
+                )
+
+        def turn_back(b, u, bank):
+            words = z_rows[b][u][:].bitcast(F32)
+            for w in range(2):
+                nc.tensor.transpose(bank[:, w * P : (w + 1) * P], words[:, w * P : (w + 1) * P], ident[:])
+
+        def quantize_z(b, u, bank, copy):
+            grouped = keep.tile([P, 4 * P], BF16, name=f"z_grouped{b}_{u}", align_bytes=64)
+            copy(
+                grouped[:].bitcast(F32).rearrange("p (v w) -> p v w", w=2),
+                bank[:, : 2 * P].rearrange("p (w v) -> p v w", w=2),
+            )
+            nc.vector.quantize_mx(
+                z_codes[b][:, u * P : (u + 1) * P].bitcast(FP8X4), z_scales[b][:, u * P : (u + 1) * P], grouped[:]
+            )
+
+        def second_pass(b, u):
+            nc.tensor.matmul_mx(
+                banks[u][:, :P],
+                lhsT=w2_codes[:, b * N : (b + 1) * N].bitcast(FP8X4),
+                lhsT_scale=w2_scales[:, b * N : (b + 1) * N],
+                rhs=z_codes[b][:, u * P : (u + 1) * P].bitcast(FP8X4),
+                rhs_scale=z_scales[b][:, u * P : (u + 1) * P],
+                start=(b == 0),
+                stop=(b == 1),
+            )
+
+        nc.vector.tensor_copy(x_bytes[:], scale_store[:].indirect(offs_t[:]))
+        gather_words(0, "x_codes0")
+        gather_words(1, "x_codes1")
+        quantize_w1(0, keep, "first_weights")
+        gather_words(2, "first_weights")
+        project_first()
+        quantize_w1(1, ring, "w1_grouped")
+        project(1)
+        quantize_w1(2, ring, "w1_grouped")
+        for c in range(TILES - 1):
+            terms = gather(c, 0, VT)
+            if c + 3 < TILES:
+                quantize_w1(c + 3, ring, "w1_grouped")
+            if c + 2 < TILES:
+                project(c + 2)
+            add_turned(c, terms, 0, VT, banks[4 + (c + 1) % 2])
+            if c == 4:
+                quantize_w2()
+            if c == 5:
+                for u in range(VT):
+                    turn_back(0, u, banks[6 + u % 2])
+                    quantize_z(0, u, banks[6 + u % 2], nc.scalar.copy)
+        last = [gather(TILES - 1, u, u + 1) for u in range(VT)]
+        for u in range(VT):
+            add_turned(TILES - 1, last[u], u, u + 1, banks[u])
+        for u in range(VT):
+            turn_back(1, u, banks[4 + u])
+        for u in range(VT):
+            second_pass(0, u)
+        for u in range(VT):
+            quantize_z(1, u, banks[4 + u], nc.scalar.copy if u % 2 else nc.vector.tensor_copy)
+        for u in range(VT):
+            second_pass(1, u)
+            result = keep.tile([P, P], F32, name=f"result{u}")
+            nc.scalar.copy(result[:], banks[u][:, :P])
+            nc.sync.dma_start(out[:, u * P : (u + 1) * P], result[:])

@@ -19,7 +19,7 @@ BANK = 512
 TILES = H // P
 VT = V // P
 X_PIECES = ((0, 512), (512, 768), (768, 1024))
-W1_LOADS = ((0, 1), (1, 2), (2, 4), (4, 8))
+W1_LOADS = ((0, 1), (1, 2), (2, 4), (4, 6), (6, 8))
 
 
 def tile_picked_sage_none_p_kernel(
@@ -52,7 +52,7 @@ def tile_picked_sage_none_p_kernel(
         word_store = loads.tile([P, T], I32, name="word_store", offset=0)
         staged = loads.tile([P, 4 * H + 2 * V + 8 * N], F32, name="staged", offset=4 * T)
         w1_raw = [staged[:, 4 * a * P : 4 * b * P].rearrange("p (j c) -> p j c", j=4) for a, b in W1_LOADS]
-        gates = staged[:, 4 * H : 4 * H + 2 * V].rearrange("p (d v) -> p d v", d=2)
+        gates = [staged[:, 4 * H + d * V : 4 * H + (d + 1) * V] for d in range(2)]
         w2_raw = staged[:, 4 * H + 2 * V :].rearrange("p (b j m) -> p b j m", b=2, j=4)
 
         nc.sync.dma_start(offs_t[:], offs)
@@ -70,10 +70,12 @@ def tile_picked_sage_none_p_kernel(
             nc.sync.dma_start(w1_raw[i], w1_rows[:, :, a * P : b * P])
 
         load_w1(0)
-        nc.sync.dma_start(gates, gate.rearrange("d p v -> p d v"))
         load_w1(1)
         load_w1(2)
+        nc.sync.dma_start(gates[0], gate[0])
         load_w1(3)
+        nc.sync.dma_start(gates[1], gate[1])
+        load_w1(4)
         nc.sync.dma_start(w2_raw, w2.rearrange("(b p j) m -> p b j m", b=2, j=4))
 
         x_bytes = keep.tile([P, S], U8, name="x_bytes", align_bytes=64)
@@ -88,7 +90,7 @@ def tile_picked_sage_none_p_kernel(
         w1_codes = [keep.tile([P, P], U32, name=f"w1_codes{c}", align_bytes=64) for c in range(TILES)]
         w1_scales = [keep.tile([P, P], U8, name=f"w1_scales{c}", align_bytes=64) for c in range(TILES)]
         h = [keep.tile([P, S], F32, name=f"h{c}") for c in range(TILES)]
-        z_rows = [[keep.tile([P, BANK], BF16, name=f"z_rows{b}_{u}") for u in range(VT)] for b in range(2)]
+        z_rows = [keep.tile([P, VT * BANK], BF16, name=f"z_rows{b}") for b in range(2)]
         z_codes = [keep.tile([P, V], U32, name=f"z_codes{b}", align_bytes=64) for b in range(2)]
         z_scales = [keep.tile([P, V], U8, name=f"z_scales{b}", align_bytes=64) for b in range(2)]
         w2_codes = keep.tile([P, 2 * N], U32, name="w2_codes", align_bytes=64)
@@ -98,14 +100,20 @@ def tile_picked_sage_none_p_kernel(
             i = max(n for n, (a, b) in enumerate(W1_LOADS) if a <= c)
             col = (c - W1_LOADS[i][0]) * P
             grouped = pool.tile([P, P, 4], BF16, name="w1_grouped", tag=tag, align_bytes=64)
-            nc.scalar.copy(grouped[:], w1_raw[i][:, :, col : col + P].rearrange("p j c -> p c j"))
+            nc.scalar.copy(
+                grouped[:].rearrange("p (c i) j -> p c j i", i=4),
+                w1_raw[i][:, :, col : col + P].rearrange("p j (c i) -> p c j i", i=4),
+            )
             nc.vector.quantize_mx(
                 w1_codes[c][:].bitcast(FP8X4), w1_scales[c][:], grouped[:].rearrange("p c j -> p (c j)")
             )
 
         def quantize_w2():
             grouped = keep.tile([P, 2, N, 4], BF16, name="w2_grouped", align_bytes=64)
-            nc.scalar.copy(grouped[:], w2_raw.rearrange("p b j m -> p b m j"))
+            nc.scalar.copy(
+                grouped[:].rearrange("p b (m i) j -> p b m j i", i=4),
+                w2_raw.rearrange("p b j (m i) -> p b m j i", i=4),
+            )
             nc.vector.quantize_mx(
                 w2_codes[:].bitcast(FP8X4), w2_scales[:], grouped[:].rearrange("p b m j -> p (b m j)")
             )
@@ -145,7 +153,7 @@ def tile_picked_sage_none_p_kernel(
                 nc.vector.tensor_tensor(
                     term[:],
                     h[c][:].indirect(pos_t[d][:, 8 * u0 : 8 * u1]),
-                    gates[:, d, u0 * P : u1 * P],
+                    gates[d][:, u0 * P : u1 * P],
                     MULT,
                 )
                 terms.append(term)
@@ -162,15 +170,14 @@ def tile_picked_sage_none_p_kernel(
                         stop=(d == 1),
                         is_transpose=True,
                     )
-            for u in range(u0, u1):
-                dst = z_rows[c // 4][u][:].rearrange("v (w q e) -> v w q e", w=2, e=2)
-                nc.scalar.copy(
-                    dst[:, :, 32 * (c % 4) : 32 * (c % 4 + 1), :],
-                    bank[:, (u - u0) * P : (u - u0 + 1) * P].rearrange("v (q w e) -> v w q e", w=2, e=2),
-                )
+            dst = z_rows[c // 4][:, u0 * BANK : u1 * BANK].rearrange("v (u w q e) -> v u w q e", w=2, q=P, e=2)
+            nc.scalar.copy(
+                dst[:, :, :, 32 * (c % 4) : 32 * (c % 4 + 1), :],
+                bank[:, : (u1 - u0) * P].rearrange("v (u q w e) -> v u w q e", q=32, w=2, e=2),
+            )
 
         def turn_back(b, u, bank):
-            words = z_rows[b][u][:].bitcast(F32)
+            words = z_rows[b][:, u * BANK : (u + 1) * BANK].bitcast(F32)
             for w in range(2):
                 nc.tensor.transpose(bank[:, w * P : (w + 1) * P], words[:, w * P : (w + 1) * P], ident[:])
 
@@ -184,9 +191,9 @@ def tile_picked_sage_none_p_kernel(
                 z_codes[b][:, u * P : (u + 1) * P].bitcast(FP8X4), z_scales[b][:, u * P : (u + 1) * P], grouped[:]
             )
 
-        def second_pass(b, u):
+        def second_pass(b, u, bank):
             nc.tensor.matmul_mx(
-                banks[u][:, :P],
+                bank[:, :P],
                 lhsT=w2_codes[:, b * N : (b + 1) * N].bitcast(FP8X4),
                 lhsT_scale=w2_scales[:, b * N : (b + 1) * N],
                 rhs=z_codes[b][:, u * P : (u + 1) * P].bitcast(FP8X4),
@@ -204,30 +211,32 @@ def tile_picked_sage_none_p_kernel(
         quantize_w1(1, ring, "w1_grouped")
         project(1)
         quantize_w1(2, ring, "w1_grouped")
+        quantize_w1(3, ring, "w1_grouped")
         for c in range(TILES - 1):
             terms = gather(c, 0, VT)
-            if c + 3 < TILES:
-                quantize_w1(c + 3, ring, "w1_grouped")
+            if c + 4 < TILES:
+                quantize_w1(c + 4, ring, "w1_grouped")
             if c + 2 < TILES:
                 project(c + 2)
-            add_turned(c, terms, 0, VT, banks[4 + (c + 1) % 2])
-            if c == 4:
-                quantize_w2()
+            add_turned(c, terms, 0, VT, banks[2 * (c % 2)])
             if c == 5:
                 for u in range(VT):
-                    turn_back(0, u, banks[6 + u % 2])
-                    quantize_z(0, u, banks[6 + u % 2], nc.scalar.copy)
+                    turn_back(0, u, banks[4 + u])
+                    quantize_z(0, u, banks[4 + u], nc.scalar.copy)
+                quantize_w2()
         last = [gather(TILES - 1, u, u + 1) for u in range(VT)]
+        sum_banks = [banks[i] for i in (2, 4, 5, 0)]
+        word_banks = [banks[i] for i in (1, 3, 6, 7)]
         for u in range(VT):
-            add_turned(TILES - 1, last[u], u, u + 1, banks[u])
+            add_turned(TILES - 1, last[u], u, u + 1, sum_banks[u])
         for u in range(VT):
-            turn_back(1, u, banks[4 + u])
+            turn_back(1, u, word_banks[u])
         for u in range(VT):
-            second_pass(0, u)
+            second_pass(0, u, sum_banks[u])
         for u in range(VT):
-            quantize_z(1, u, banks[4 + u], nc.scalar.copy if u % 2 else nc.vector.tensor_copy)
+            quantize_z(1, u, word_banks[u], nc.scalar.copy if u % 2 else nc.vector.tensor_copy)
         for u in range(VT):
-            second_pass(1, u)
+            second_pass(1, u, sum_banks[u])
             result = keep.tile([P, P], F32, name=f"result{u}")
-            nc.scalar.copy(result[:], banks[u][:, :P])
+            nc.scalar.copy(result[:], sum_banks[u][:, :P])
             nc.sync.dma_start(out[:, u * P : (u + 1) * P], result[:])

@@ -12,14 +12,20 @@ U32 = mybir.dt.uint32
 U16 = mybir.dt.uint16
 U8 = mybir.dt.uint8
 FP8X4 = mybir.dt.float8_e4m3fn_x4
-MULT = mybir.AluOpType.mult
 
 P = 128
+PACK = 4
 BANK = 512
+STRIPE = 16
 TILES = H // P
-VT = V // P
-X_PIECES = ((0, 512), (512, 768), (768, 1024))
-W1_LOADS = ((0, 1), (1, 2), (2, 4), (4, 6), (6, 8))
+PASSES = H // (P * PACK)
+TILES_A_PASS = TILES // PASSES
+GROUPS = V // P
+RING = 4
+PRODUCTS_AHEAD = 2
+WEIGHTS_AHEAD = 4
+WORD_PIECES = ((0, 512), (512, 768), (768, 1024))
+W1_LOADS = ((0, 1), (1, 2), (2, 3), (3, 4), (4, 6), (6, 8))
 
 
 def tile_picked_sage_none_p_kernel(
@@ -29,19 +35,20 @@ def tile_picked_sage_none_p_kernel(
     with ExitStack() as ctx:
         keep = ctx.enter_context(tc.tile_pool(name="keep", bufs=1))
         loads = ctx.enter_context(tc.tile_pool(name="loads", bufs=1))
-        ring = ctx.enter_context(tc.tile_pool(name="ring", bufs=4))
+        ring = ctx.enter_context(tc.tile_pool(name="ring", bufs=RING))
         psum = ctx.enter_context(tc.psum_pool(name="psum", bufs=1))
         banks = [psum.tile([P, BANK], F32, name=f"bank{i}") for i in range(8)]
 
-        offs_t = keep.tile([P, S // 16], U16, name="offs_t")
-        pos_t = [keep.tile([P, V // 16], U16, name=f"pos{d}_t") for d in range(2)]
+        offs_list = keep.tile([P, S // STRIPE], U16, name="offs_list")
+        pos_lists = [keep.tile([P, V // STRIPE], U16, name=f"pos{d}_list") for d in range(2)]
+
         scale_store = keep.tile([P, T], U8, name="scale_store")
-        ident = keep.tile([P, P], F32, name="ident")
+        identity = keep.tile([P, P], F32, name="identity")
         zeros = loads.tile([P, P], F32, name="zeros", offset=4 * T - 2 * P)
         nc.vector.memset(scale_store[:].bitcast(I32), 0)
         nc.gpsimd.memset(zeros[:], 0.0)
         nc.gpsimd.affine_select(
-            out=ident[:],
+            out=identity[:],
             in_=zeros[:],
             compare_op=mybir.AluOpType.not_equal,
             fill=1.0,
@@ -50,56 +57,49 @@ def tile_picked_sage_none_p_kernel(
             channel_multiplier=1,
         )
         word_store = loads.tile([P, T], I32, name="word_store", offset=0)
-        staged = loads.tile([P, 4 * H + 2 * V + 8 * N], F32, name="staged", offset=4 * T)
-        w1_raw = [staged[:, 4 * a * P : 4 * b * P].rearrange("p (j c) -> p j c", j=4) for a, b in W1_LOADS]
-        gates = [staged[:, 4 * H + d * V : 4 * H + (d + 1) * V] for d in range(2)]
-        w2_raw = staged[:, 4 * H + 2 * V :].rearrange("p (b j m) -> p b j m", b=2, j=4)
+        w1_width, gate_width, w2_width = PACK * H, 2 * V, PASSES * PACK * N
+        staged = loads.tile([P, w1_width + gate_width + w2_width], F32, name="staged", offset=4 * T)
+        w1_raw = [staged[:, PACK * a * P : PACK * b * P].rearrange("p (j c) -> p j c", j=PACK) for a, b in W1_LOADS]
+        gates = [staged[:, w1_width + d * V : w1_width + (d + 1) * V] for d in range(2)]
+        w2_raw = staged[:, w1_width + gate_width :].rearrange("p (b j m) -> p b j m", b=PASSES, j=PACK)
 
-        nc.sync.dma_start(offs_t[:], offs)
-        nc.sync.dma_start(pos_t[0][:], pos1)
-        nc.sync.dma_start(pos_t[1][:], pos2)
+        nc.sync.dma_start(offs_list[:], offs)
+        nc.sync.dma_start(pos_lists[0][:], pos1)
+        nc.sync.dma_start(pos_lists[1][:], pos2)
         for q in range(4):
             nc.sync.dma_start(
                 scale_store[32 * q : 32 * q + 4, :].bitcast(I32), x_scales[0, 4 * q : 4 * q + 4, :].bitcast(I32)
             )
-        nc.sync.dma_start(word_store[:], x_words[0].rearrange("p c r -> p (c r)").bitcast(I32))
-        w1_rows = w1.rearrange("(p j) c -> p j c", j=4)
+        w1_rows = w1.rearrange("(p j) c -> p j c", j=PACK)
 
         def load_w1(i):
             a, b = W1_LOADS[i]
             nc.sync.dma_start(w1_raw[i], w1_rows[:, :, a * P : b * P])
 
         load_w1(0)
-        load_w1(1)
-        load_w1(2)
-        nc.sync.dma_start(gates[0], gate[0])
-        load_w1(3)
-        nc.sync.dma_start(gates[1], gate[1])
-        load_w1(4)
-        nc.sync.dma_start(w2_raw, w2.rearrange("(b p j) m -> p b j m", b=2, j=4))
+        nc.sync.dma_start(word_store[:], x_words[0].rearrange("p c r -> p (c r)").bitcast(I32))
+        for d in range(2):
+            load_w1(1 + d)
+            nc.sync.dma_start(gates[d], gate[d])
+        for i in range(3, len(W1_LOADS)):
+            load_w1(i)
+        nc.sync.dma_start(w2_raw, w2.rearrange("(b p j) m -> p b j m", b=PASSES, j=PACK))
 
         x_bytes = keep.tile([P, S], U8, name="x_bytes", align_bytes=64)
-        x_codes = []
-
-        def gather_words(i, tag):
-            a, b = X_PIECES[i]
-            codes = keep.tile([P, b - a], U32, name=f"x_codes{i}", tag=tag, align_bytes=64)
-            nc.vector.tensor_copy(codes[:], word_store[:].bitcast(U32).indirect(offs_t[:, a // 16 : b // 16]))
-            x_codes.append(codes)
-
+        x_codes = keep.tile([P, S], U32, name="x_codes", align_bytes=64)
         w1_codes = [keep.tile([P, P], U32, name=f"w1_codes{c}", align_bytes=64) for c in range(TILES)]
         w1_scales = [keep.tile([P, P], U8, name=f"w1_scales{c}", align_bytes=64) for c in range(TILES)]
         h = [keep.tile([P, S], F32, name=f"h{c}") for c in range(TILES)]
-        z_rows = [keep.tile([P, VT * BANK], BF16, name=f"z_rows{b}") for b in range(2)]
-        z_codes = [keep.tile([P, V], U32, name=f"z_codes{b}", align_bytes=64) for b in range(2)]
-        z_scales = [keep.tile([P, V], U8, name=f"z_scales{b}", align_bytes=64) for b in range(2)]
-        w2_codes = keep.tile([P, 2 * N], U32, name="w2_codes", align_bytes=64)
-        w2_scales = keep.tile([P, 2 * N], U8, name="w2_scales", align_bytes=64)
+        z_rows = [[keep.tile([P, BANK], BF16, name=f"z_rows{b}_{u}") for u in range(GROUPS)] for b in range(PASSES)]
+        z_codes = [keep.tile([P, V], U32, name=f"z_codes{b}", align_bytes=64) for b in range(PASSES)]
+        z_scales = [keep.tile([P, V], U8, name=f"z_scales{b}", align_bytes=64) for b in range(PASSES)]
+        w2_codes = keep.tile([P, PASSES * N], U32, name="w2_codes", align_bytes=64)
+        w2_scales = keep.tile([P, PASSES * N], U8, name="w2_scales", align_bytes=64)
 
-        def quantize_w1(c, pool, tag):
+        def quantize_w1(c):
             i = max(n for n, (a, b) in enumerate(W1_LOADS) if a <= c)
             col = (c - W1_LOADS[i][0]) * P
-            grouped = pool.tile([P, P, 4], BF16, name="w1_grouped", tag=tag, align_bytes=64)
+            grouped = ring.tile([P, P, PACK], BF16, name="w1_grouped", align_bytes=64)
             nc.scalar.copy(
                 grouped[:].rearrange("p (c i) j -> p c j i", i=4),
                 w1_raw[i][:, :, col : col + P].rearrange("p j (c i) -> p c j i", i=4),
@@ -109,7 +109,7 @@ def tile_picked_sage_none_p_kernel(
             )
 
         def quantize_w2():
-            grouped = keep.tile([P, 2, N, 4], BF16, name="w2_grouped", align_bytes=64)
+            grouped = keep.tile([P, PASSES, N, PACK], BF16, name="w2_grouped", align_bytes=64)
             nc.scalar.copy(
                 grouped[:].rearrange("p b (m i) j -> p b m j i", i=4),
                 w2_raw.rearrange("p b j (m i) -> p b m j i", i=4),
@@ -118,80 +118,72 @@ def tile_picked_sage_none_p_kernel(
                 w2_codes[:].bitcast(FP8X4), w2_scales[:], grouped[:].rearrange("p b m j -> p (b m j)")
             )
 
-        def multiply(c, i, dst):
-            a, b = X_PIECES[i]
+        def first_product(c, a, b, dst):
             nc.tensor.matmul_mx(
                 dst,
                 lhsT=w1_codes[c][:].bitcast(FP8X4),
                 lhsT_scale=w1_scales[c][:],
-                rhs=x_codes[i][:].bitcast(FP8X4),
+                rhs=x_codes[:, a:b].bitcast(FP8X4),
                 rhs_scale=x_bytes[:, a:b],
                 start=True,
                 stop=True,
             )
 
         def project(c):
-            low, high = banks[2 * (c % 2)], banks[2 * (c % 2) + 1]
-            multiply(c, 0, low[:])
-            nc.scalar.copy(h[c][:, :BANK], low[:])
-            multiply(c, 1, high[:, :256])
-            multiply(c, 2, high[:, 256:])
-            nc.scalar.copy(h[c][:, BANK:], high[:])
+            for i in range(2):
+                bank = banks[2 * (c % 2) + i]
+                first_product(c, i * BANK, (i + 1) * BANK, bank[:])
+                nc.scalar.copy(h[c][:, i * BANK : (i + 1) * BANK], bank[:])
 
         def project_first():
-            multiply(0, 0, banks[0][:])
-            nc.scalar.copy(h[0][:, :BANK], banks[0][:])
-            multiply(0, 1, banks[1][:, :256])
-            nc.scalar.copy(h[0][:, 512:768], banks[1][:, :256])
-            multiply(0, 2, banks[4][:, :256])
-            nc.vector.tensor_copy(h[0][:, 768:], banks[4][:, :256])
+            for (a, b), bank in zip(WORD_PIECES, (banks[0], banks[1], banks[4])):
+                first_product(0, a, b, bank[:, : b - a])
+                copy = nc.vector.tensor_copy if b == S else nc.scalar.copy
+                copy(h[0][:, a:b], bank[:, : b - a])
 
-        def gather(c, u0, u1):
+        def gather_terms(c, u0, u1):
             terms = []
             for d in range(2):
                 term = ring.tile([P, (u1 - u0) * P], F32, name=f"term{d}")
                 nc.vector.tensor_tensor(
                     term[:],
-                    h[c][:].indirect(pos_t[d][:, 8 * u0 : 8 * u1]),
+                    h[c][:].indirect(pos_lists[d][:, u0 * P // STRIPE : u1 * P // STRIPE]),
                     gates[d][:, u0 * P : u1 * P],
-                    MULT,
+                    mybir.AluOpType.mult,
                 )
                 terms.append(term)
             return terms
 
-        def add_turned(c, terms, u0, u1, bank):
-            for u in range(u0, u1):
+        def add_turned(terms, sums):
+            for u in range(sums.shape[1] // P):
+                cols = slice(u * P, (u + 1) * P)
                 for d in range(2):
                     nc.tensor.matmul(
-                        bank[:, (u - u0) * P : (u - u0 + 1) * P],
-                        lhsT=terms[d][:, (u - u0) * P : (u - u0 + 1) * P],
-                        rhs=ident[:],
+                        sums[:, cols],
+                        lhsT=terms[d][:, cols],
+                        rhs=identity[:],
                         start=(d == 0),
                         stop=(d == 1),
                         is_transpose=True,
                     )
-            dst = z_rows[c // 4][:, u0 * BANK : u1 * BANK].rearrange("v (u w q e) -> v u w q e", w=2, q=P, e=2)
-            nc.scalar.copy(
-                dst[:, :, :, 32 * (c % 4) : 32 * (c % 4 + 1), :],
-                bank[:, : (u1 - u0) * P].rearrange("v (u q w e) -> v u w q e", q=32, w=2, e=2),
-            )
+
+        def round_sums(c, u, sums):
+            first = 32 * (c % TILES_A_PASS)
+            dst = z_rows[c // TILES_A_PASS][u][:].rearrange("v (w p e) -> v w p e", w=2, e=2)
+            nc.scalar.copy(dst[:, :, first : first + 32, :], sums.rearrange("v (p w e) -> v w p e", w=2, e=2))
 
         def turn_back(b, u, bank):
-            words = z_rows[b][:, u * BANK : (u + 1) * BANK].bitcast(F32)
+            words = z_rows[b][u][:].bitcast(F32)
             for w in range(2):
-                nc.tensor.transpose(bank[:, w * P : (w + 1) * P], words[:, w * P : (w + 1) * P], ident[:])
+                nc.tensor.transpose(bank[:, w * P : (w + 1) * P], words[:, w * P : (w + 1) * P], identity[:])
 
-        def quantize_z(b, u, bank, copy):
-            grouped = keep.tile([P, 4 * P], BF16, name=f"z_grouped{b}_{u}", align_bytes=64)
-            copy(
-                grouped[:].bitcast(F32).rearrange("p (v w) -> p v w", w=2),
+        def interleave(dst, bank):
+            nc.scalar.copy(
+                dst.bitcast(F32).rearrange("p (v w) -> p v w", w=2),
                 bank[:, : 2 * P].rearrange("p (w v) -> p v w", w=2),
             )
-            nc.vector.quantize_mx(
-                z_codes[b][:, u * P : (u + 1) * P].bitcast(FP8X4), z_scales[b][:, u * P : (u + 1) * P], grouped[:]
-            )
 
-        def second_pass(b, u, bank):
+        def second_product(b, u, bank):
             nc.tensor.matmul_mx(
                 bank[:, :P],
                 lhsT=w2_codes[:, b * N : (b + 1) * N].bitcast(FP8X4),
@@ -199,44 +191,66 @@ def tile_picked_sage_none_p_kernel(
                 rhs=z_codes[b][:, u * P : (u + 1) * P].bitcast(FP8X4),
                 rhs_scale=z_scales[b][:, u * P : (u + 1) * P],
                 start=(b == 0),
-                stop=(b == 1),
+                stop=(b == PASSES - 1),
             )
 
-        nc.vector.tensor_copy(x_bytes[:], scale_store[:].indirect(offs_t[:]))
-        gather_words(0, "x_codes0")
-        gather_words(1, "x_codes1")
-        quantize_w1(0, keep, "first_weights")
-        gather_words(2, "first_weights")
+        nc.vector.tensor_copy(x_bytes[:], scale_store[:].indirect(offs_list[:]))
+        quantize_w1(0)
+        for a, b in WORD_PIECES:
+            nc.vector.tensor_copy(
+                x_codes[:, a:b], word_store[:].bitcast(U32).indirect(offs_list[:, a // STRIPE : b // STRIPE])
+            )
+        quantize_w1(1)
         project_first()
-        quantize_w1(1, ring, "w1_grouped")
+        quantize_w1(2)
         project(1)
-        quantize_w1(2, ring, "w1_grouped")
-        quantize_w1(3, ring, "w1_grouped")
+        quantize_w1(3)
+
         for c in range(TILES - 1):
-            terms = gather(c, 0, VT)
-            if c + 4 < TILES:
-                quantize_w1(c + 4, ring, "w1_grouped")
-            if c + 2 < TILES:
-                project(c + 2)
-            add_turned(c, terms, 0, VT, banks[2 * (c % 2)])
-            if c == 5:
-                for u in range(VT):
+            terms = gather_terms(c, 0, GROUPS)
+            if c + WEIGHTS_AHEAD < TILES:
+                quantize_w1(c + WEIGHTS_AHEAD)
+            if c + PRODUCTS_AHEAD < TILES:
+                project(c + PRODUCTS_AHEAD)
+            sum_bank = banks[2 * (c % 2)]
+            add_turned(terms, sum_bank[:])
+            for u in range(GROUPS):
+                round_sums(c, u, sum_bank[:, u * P : (u + 1) * P])
+            if c == TILES - PRODUCTS_AHEAD - 1:
+                z_first = keep.tile([P, PACK * V], BF16, name="z_first", align_bytes=64)
+                for u in range(GROUPS):
                     turn_back(0, u, banks[4 + u])
-                    quantize_z(0, u, banks[4 + u], nc.scalar.copy)
+                    interleave(z_first[:, u * BANK : (u + 1) * BANK], banks[4 + u])
+                nc.vector.quantize_mx(z_codes[0][:].bitcast(FP8X4), z_scales[0][:], z_first[:])
                 quantize_w2()
-        last = [gather(TILES - 1, u, u + 1) for u in range(VT)]
-        sum_banks = [banks[i] for i in (2, 4, 5, 0)]
+
+        last_terms = [gather_terms(TILES - 1, u, u + 1) for u in range(GROUPS)]
+
+        out_banks = [banks[i] for i in (2, 4, 5, 0)]
         word_banks = [banks[i] for i in (1, 3, 6, 7)]
-        for u in range(VT):
-            add_turned(TILES - 1, last[u], u, u + 1, sum_banks[u])
-        for u in range(VT):
+        last_sums = [bank[:, :P] for bank in out_banks[:2]] + [bank[:, 2 * P : 3 * P] for bank in word_banks[:2]]
+
+        def quantize_last(u):
+            grouped = keep.tile([P, PACK * P], BF16, name=f"z_last{u}", align_bytes=64)
+            interleave(grouped[:], word_banks[u])
+            cols = slice(u * P, (u + 1) * P)
+            nc.vector.quantize_mx(z_codes[1][:, cols].bitcast(FP8X4), z_scales[1][:, cols], grouped[:])
+
+        for u in range(GROUPS):
+            if u >= 2:
+                turn_back(1, u - 2, word_banks[u - 2])
+            add_turned(last_terms[u], last_sums[u])
+            round_sums(TILES - 1, u, last_sums[u])
+            if u >= 2:
+                quantize_last(u - 2)
+        for u in range(2, GROUPS):
             turn_back(1, u, word_banks[u])
-        for u in range(VT):
-            second_pass(0, u, sum_banks[u])
-        for u in range(VT):
-            quantize_z(1, u, word_banks[u], nc.scalar.copy if u % 2 else nc.vector.tensor_copy)
-        for u in range(VT):
-            second_pass(1, u, sum_banks[u])
+            quantize_last(u)
+
+        for u in range(GROUPS):
+            second_product(0, u, out_banks[u])
+        for u in range(GROUPS):
+            second_product(1, u, out_banks[u])
             result = keep.tile([P, P], F32, name=f"result{u}")
-            nc.scalar.copy(result[:], sum_banks[u][:, :P])
+            nc.scalar.copy(result[:], out_banks[u][:, :P])
             nc.sync.dma_start(out[:, u * P : (u + 1) * P], result[:])

from contextlib import ExitStack

import concourse.mybir as mybir

K, T, S, V, H, N = 512, 2048, 1024, 512, 1024, 128
FLOPS = 2 * K * H * S + 2 * H * N * V

F32 = mybir.dt.float32
BF16 = mybir.dt.bfloat16
I32 = mybir.dt.int32
U32 = mybir.dt.uint32
U16 = mybir.dt.uint16
U8 = mybir.dt.uint8
FP8X4 = mybir.dt.float8_e4m3fn_x4

P = 128
PACK = 4
BANK = 512
STRIPE = 16
TILES = H // P
PASSES = H // (P * PACK)
TILES_A_PASS = TILES // PASSES
GROUPS = V // P
RING = 4
PRODUCTS_AHEAD = 2
WEIGHTS_AHEAD = 4
WORD_PIECES = ((0, 512), (512, 768), (768, 1024))
W1_LOADS = ((0, 1), (1, 2), (2, 3), (3, 4), (4, 6), (6, 8))


def tile_picked_sage_none_p_kernel(
    tc, x_words, x_scales, w1, w2, gate, offs, pos1, pos2, out
):
    nc = tc.nc
    with ExitStack() as ctx:
        keep = ctx.enter_context(tc.tile_pool(name="keep", bufs=1))
        loads = ctx.enter_context(tc.tile_pool(name="loads", bufs=1))
        ring = ctx.enter_context(tc.tile_pool(name="ring", bufs=RING))
        psum = ctx.enter_context(tc.psum_pool(name="psum", bufs=1))
        banks = [psum.tile([P, BANK], F32, name=f"bank{i}") for i in range(8)]

        offs_list = keep.tile([P, S // STRIPE], U16, name="offs_list")
        pos_lists = [keep.tile([P, V // STRIPE], U16, name=f"pos{d}_list") for d in range(2)]

        scale_store = keep.tile([P, T], U8, name="scale_store")
        identity = keep.tile([P, P], F32, name="identity")
        zeros = loads.tile([P, P], F32, name="zeros", offset=4 * T - 2 * P)
        nc.vector.memset(scale_store[:].bitcast(I32), 0)
        nc.gpsimd.memset(zeros[:], 0.0)
        nc.gpsimd.affine_select(
            out=identity[:],
            in_=zeros[:],
            compare_op=mybir.AluOpType.not_equal,
            fill=1.0,
            base=0,
            pattern=[[-1, P]],
            channel_multiplier=1,
        )
        word_store = loads.tile([P, T], I32, name="word_store", offset=0)
        w1_width, gate_width, w2_width = PACK * H, 2 * V, PASSES * PACK * N
        staged = loads.tile([P, w1_width + gate_width + w2_width], F32, name="staged", offset=4 * T)
        w1_raw = [staged[:, PACK * a * P : PACK * b * P].rearrange("p (j c) -> p j c", j=PACK) for a, b in W1_LOADS]
        gates = [staged[:, w1_width + d * V : w1_width + (d + 1) * V] for d in range(2)]
        w2_raw = staged[:, w1_width + gate_width :].rearrange("p (b j m) -> p b j m", b=PASSES, j=PACK)

        nc.sync.dma_start(offs_list[:], offs)
        nc.sync.dma_start(pos_lists[0][:], pos1)
        nc.sync.dma_start(pos_lists[1][:], pos2)
        for q in range(4):
            nc.sync.dma_start(
                scale_store[32 * q : 32 * q + 4, :].bitcast(I32), x_scales[0, 4 * q : 4 * q + 4, :].bitcast(I32)
            )
        w1_rows = w1.rearrange("(p j) c -> p j c", j=PACK)

        def load_w1(i):
            a, b = W1_LOADS[i]
            nc.sync.dma_start(w1_raw[i], w1_rows[:, :, a * P : b * P])

        load_w1(0)
        nc.sync.dma_start(word_store[:], x_words[0].rearrange("p c r -> p (c r)").bitcast(I32))
        for d in range(2):
            load_w1(1 + d)
            nc.sync.dma_start(gates[d], gate[d])
        for i in range(3, len(W1_LOADS)):
            load_w1(i)
        nc.sync.dma_start(w2_raw, w2.rearrange("(b p j) m -> p b j m", b=PASSES, j=PACK))

        x_bytes = keep.tile([P, S], U8, name="x_bytes", align_bytes=64)
        x_codes = keep.tile([P, S], U32, name="x_codes", align_bytes=64)
        w1_codes = [keep.tile([P, P], U32, name=f"w1_codes{c}", align_bytes=64) for c in range(TILES)]
        w1_scales = [keep.tile([P, P], U8, name=f"w1_scales{c}", align_bytes=64) for c in range(TILES)]
        h = [keep.tile([P, S], F32, name=f"h{c}") for c in range(TILES)]
        z_rows = [[keep.tile([P, BANK], BF16, name=f"z_rows{b}_{u}") for u in range(GROUPS)] for b in range(PASSES)]
        z_codes = [keep.tile([P, V], U32, name=f"z_codes{b}", align_bytes=64) for b in range(PASSES)]
        z_scales = [keep.tile([P, V], U8, name=f"z_scales{b}", align_bytes=64) for b in range(PASSES)]
        w2_codes = keep.tile([P, PASSES * N], U32, name="w2_codes", align_bytes=64)
        w2_scales = keep.tile([P, PASSES * N], U8, name="w2_scales", align_bytes=64)

        def quantize_w1(c):
            i = max(n for n, (a, b) in enumerate(W1_LOADS) if a <= c)
            col = (c - W1_LOADS[i][0]) * P
            grouped = ring.tile([P, P, PACK], BF16, name="w1_grouped", align_bytes=64)
            nc.scalar.copy(
                grouped[:].rearrange("p (c i) j -> p c j i", i=4),
                w1_raw[i][:, :, col : col + P].rearrange("p j (c i) -> p c j i", i=4),
            )
            nc.vector.quantize_mx(
                w1_codes[c][:].bitcast(FP8X4), w1_scales[c][:], grouped[:].rearrange("p c j -> p (c j)")
            )

        def quantize_w2():
            grouped = keep.tile([P, PASSES, N, PACK], BF16, name="w2_grouped", align_bytes=64)
            nc.scalar.copy(
                grouped[:].rearrange("p b (m i) j -> p b m j i", i=4),
                w2_raw.rearrange("p b j (m i) -> p b m j i", i=4),
            )
            nc.vector.quantize_mx(
                w2_codes[:].bitcast(FP8X4), w2_scales[:], grouped[:].rearrange("p b m j -> p (b m j)")
            )

        def first_product(c, a, b, dst):
            nc.tensor.matmul_mx(
                dst,
                lhsT=w1_codes[c][:].bitcast(FP8X4),
                lhsT_scale=w1_scales[c][:],
                rhs=x_codes[:, a:b].bitcast(FP8X4),
                rhs_scale=x_bytes[:, a:b],
                start=True,
                stop=True,
            )

        def project(c):
            for i in range(2):
                bank = banks[2 * (c % 2) + i]
                first_product(c, i * BANK, (i + 1) * BANK, bank[:])
                nc.scalar.copy(h[c][:, i * BANK : (i + 1) * BANK], bank[:])

        def project_first():
            for (a, b), bank in zip(WORD_PIECES, (banks[0], banks[1], banks[4])):
                first_product(0, a, b, bank[:, : b - a])
                copy = nc.vector.tensor_copy if b == S else nc.scalar.copy
                copy(h[0][:, a:b], bank[:, : b - a])

        def gather_terms(c, u0, u1):
            terms = []
            for d in range(2):
                term = ring.tile([P, (u1 - u0) * P], F32, name=f"term{d}")
                nc.vector.tensor_tensor(
                    term[:],
                    h[c][:].indirect(pos_lists[d][:, u0 * P // STRIPE : u1 * P // STRIPE]),
                    gates[d][:, u0 * P : u1 * P],
                    mybir.AluOpType.mult,
                )
                terms.append(term)
            return terms

        def add_turned(terms, sums):
            for u in range(sums.shape[1] // P):
                cols = slice(u * P, (u + 1) * P)
                for d in range(2):
                    nc.tensor.matmul(
                        sums[:, cols],
                        lhsT=terms[d][:, cols],
                        rhs=identity[:],
                        start=(d == 0),
                        stop=(d == 1),
                        is_transpose=True,
                    )

        def round_sums(c, u, sums):
            first = 32 * (c % TILES_A_PASS)
            dst = z_rows[c // TILES_A_PASS][u][:].rearrange("v (w p e) -> v w p e", w=2, e=2)
            nc.scalar.copy(dst[:, :, first : first + 32, :], sums.rearrange("v (p w e) -> v w p e", w=2, e=2))

        def turn_back(b, u, bank):
            words = z_rows[b][u][:].bitcast(F32)
            for w in range(2):
                nc.tensor.transpose(bank[:, w * P : (w + 1) * P], words[:, w * P : (w + 1) * P], identity[:])

        def interleave(dst, bank):
            nc.scalar.copy(
                dst.bitcast(F32).rearrange("p (v w) -> p v w", w=2),
                bank[:, : 2 * P].rearrange("p (w v) -> p v w", w=2),
            )

        def second_product(b, u, bank):
            nc.tensor.matmul_mx(
                bank[:, :P],
                lhsT=w2_codes[:, b * N : (b + 1) * N].bitcast(FP8X4),
                lhsT_scale=w2_scales[:, b * N : (b + 1) * N],
                rhs=z_codes[b][:, u * P : (u + 1) * P].bitcast(FP8X4),
                rhs_scale=z_scales[b][:, u * P : (u + 1) * P],
                start=(b == 0),
                stop=(b == PASSES - 1),
            )

        nc.vector.tensor_copy(x_bytes[:], scale_store[:].indirect(offs_list[:]))
        quantize_w1(0)
        for a, b in WORD_PIECES:
            nc.vector.tensor_copy(
                x_codes[:, a:b], word_store[:].bitcast(U32).indirect(offs_list[:, a // STRIPE : b // STRIPE])
            )
        quantize_w1(1)
        project_first()
        quantize_w1(2)
        project(1)
        quantize_w1(3)

        for c in range(TILES - 1):
            terms = gather_terms(c, 0, GROUPS)
            if c + WEIGHTS_AHEAD < TILES:
                quantize_w1(c + WEIGHTS_AHEAD)
            if c + PRODUCTS_AHEAD < TILES:
                project(c + PRODUCTS_AHEAD)
            sum_bank = banks[2 * (c % 2)]
            add_turned(terms, sum_bank[:])
            for u in range(GROUPS):
                round_sums(c, u, sum_bank[:, u * P : (u + 1) * P])
            if c == TILES - PRODUCTS_AHEAD - 1:
                z_first = keep.tile([P, PACK * V], BF16, name="z_first", align_bytes=64)
                for u in range(GROUPS):
                    turn_back(0, u, banks[4 + u])
                    interleave(z_first[:, u * BANK : (u + 1) * BANK], banks[4 + u])
                nc.vector.quantize_mx(z_codes[0][:].bitcast(FP8X4), z_scales[0][:], z_first[:])
                quantize_w2()

        last_terms = [gather_terms(TILES - 1, u, u + 1) for u in range(GROUPS)]

        out_banks = [banks[i] for i in (2, 4, 5, 0)]
        word_banks = [banks[i] for i in (1, 3, 6, 7)]
        last_sums = [bank[:, :P] for bank in out_banks[:2]] + [bank[:, 2 * P : 3 * P] for bank in word_banks[:2]]

        def quantize_last(u):
            grouped = keep.tile([P, PACK * P], BF16, name=f"z_last{u}", align_bytes=64)
            interleave(grouped[:], word_banks[u])
            cols = slice(u * P, (u + 1) * P)
            nc.vector.quantize_mx(z_codes[1][:, cols].bitcast(FP8X4), z_scales[1][:, cols], grouped[:])

        for u in range(GROUPS):
            if u >= 2:
                turn_back(1, u - 2, word_banks[u - 2])
            add_turned(last_terms[u], last_sums[u])
            round_sums(TILES - 1, u, last_sums[u])
            if u >= 2:
                quantize_last(u - 2)
        for u in range(2, GROUPS):
            turn_back(1, u, word_banks[u])
            quantize_last(u)

        for u in range(GROUPS):
            second_product(0, u, out_banks[u])
        for u in range(GROUPS):
            second_product(1, u, out_banks[u])
            result = keep.tile([P, P], F32, name=f"result{u}")
            nc.scalar.copy(result[:], out_banks[u][:, :P])
            nc.sync.dma_start(out[:, u * P : (u + 1) * P], result[:])
